import numpy as np, ml_dtypes
CORES = [4,20,36,52,68,84,100,116,132,148,164,180,196,212,228,244]
N = 16
F = 32
def setup_inputs(rng):
    x = (rng.standard_normal((N, 128, 128), dtype=np.float32) / 11).astype(ml_dtypes.bfloat16)
    w = rng.standard_normal((128, F), dtype=np.float32).astype(ml_dtypes.bfloat16)
    return {"x": x, "xt": x.transpose(0, 2, 1).copy(), "w": np.broadcast_to(w, (N, 128, F)).copy()}
def setup_inputs_big(rng):
    d = setup_inputs(rng)
    for k in ("x", "xt", "w"): d[k] = (d[k].astype(np.float32) * 1024.0).astype(d[k].dtype)
    return d
def setup_inputs_small(rng):
    d = setup_inputs(rng)
    for k in ("x", "xt", "w"): d[k] = (d[k].astype(np.float32) * (1 / 1024.0)).astype(d[k].dtype)
    return d
def setup_inputs_apart(rng):
    d = setup_inputs(rng)
    f = (10.0 ** rng.permutation(np.linspace(-1.5, 1.5, N))).astype(np.float32).reshape(N, 1, 1)
    for k in ("x", "xt"): d[k] = (d[k].astype(np.float32) * f).astype(d[k].dtype)
    return d
def tie_inputs(x):
    x = dict(x)
    x["xt"] = x["x"].transpose(0, 2, 1).copy(); x["w"] = np.broadcast_to(x["w"][0], x["w"].shape).copy()
    return x
def reference(x, xt, w):
    X, XT, W = x.astype(np.float64), xt.astype(np.float64), w.astype(np.float64)
    s = sum(X[j].T @ (XT[j].T @ W[j]) for j in range(N)).astype(ml_dtypes.bfloat16 if x.dtype != np.float64 else np.float64)
    return {"y": np.broadcast_to(s, (N,) + s.shape)}

from concourse.bass import DstId, RemoteDMATransfer

N = 16
F = 32
GRP = 2
NB = N // GRP
BW = F // NB

SCRATCH = {
    "x_sb": ("sbuf", [128, 128], "bfloat16"),
    "w_sb": ("sbuf", [128, F], "bfloat16"),
    "g_sb": ("sbuf", [128, 128], "bfloat16"),
    "p_sb": ("sbuf", [128, F], "bfloat16"),
    "ps_g": ("psum", [128, 512], "float32"),
    "ps_p": ("psum", [128, 512], "float32"),
    "stage": ("dram", [NB, 128, BW], "bfloat16"),
    "rsland": ("dram", [N, 128, BW], "bfloat16"),
    "agland": ("dram", [NB, 128, BW], "bfloat16"),
}
SEMAPHORES = ["ldx", "ldw", "mmg", "cpg", "mmp", "cpp", "staged", "rs", "ag", "left", "stored"]


def rank_program(g, core, T, topo):
    rank = T.rank_of(core)
    if rank is None:
        return
    sem = T.sem
    cores = T.cores
    blk, own = rank // GRP, rank % GRP

    def dst_id(k):
        rid, pid = topo.addr(cores[k], core)
        return DstId(rid=rid, pnc=pid)

    common = -1
    for k in range(N):
        if k != rank:
            common &= topo.mask(core, cores[k])
    usable = [e for e in range(common.bit_length()) if (common >> e) & 1]
    eng = [1 << usable[i * len(usable) // NB] for i in range(NB)]

    g.sync.dma_start(T.x_sb[:], T.x[:]).then_inc(sem.ldx, 16)
    g.scalar.dma_start(T.w_sb[:], T.w[:]).then_inc(sem.ldw, 16)

    g.tensor.wait_ge(sem.ldx, 16)
    g.tensor.matmul(T.ps_g[:, 0:128], T.x_sb[:], T.x_sb[:], True, True).then_inc(sem.mmg, 1)
    g.vector.wait_ge(sem.mmg, 1)
    g.vector.tensor_copy(T.g_sb[:], T.ps_g[:, 0:128]).then_inc(sem.cpg, 1)
    g.tensor.wait_ge(sem.ldw, 16)
    g.tensor.wait_ge(sem.cpg, 1)
    g.tensor.matmul(T.ps_p[:, 0:F], T.g_sb[:], T.w_sb[:], True, True).then_inc(sem.mmp, 1)
    g.vector.wait_ge(sem.mmp, 1)
    g.vector.tensor_copy(T.p_sb[:], T.ps_p[:, 0:F]).then_inc(sem.cpp, 1)

    g.sync.wait_ge(sem.cpp, 1)
    g.sync.dma_start(T.stage[:], T.p_sb[:]).then_inc(sem.staged, 16)

    g.wait_ge(sem.staged, 16)
    out = []
    for i in range(NB):
        b = (blk + i) % NB
        owners = [k for k in range(GRP * b, GRP * b + GRP) if k != rank]
        out.append(RemoteDMATransfer(dst_ids=[dst_id(k) for k in owners], dma_engine_mask=eng[i], remote_sem=sem.rs,
                                     srcs=[T.stage[b]], dsts=[T.rsland[rank] for k in owners], alu_op=0))
    g.remote_dma_fused(out, local_sem=sem.left)

    g.wait_ge(sem.rs, N - 1)
    parts = [T.stage[blk] if j == rank else T.rsland[j] for j in range(N)]
    served = [k for k in range(N) if k % GRP == (own + 1) % GRP]
    served = served[blk:] + served[:blk]
    out = [RemoteDMATransfer(dst_ids=[dst_id(k)], dma_engine_mask=eng[i], remote_sem=sem.ag,
                             srcs=parts, dsts=[T.agland[blk]], alu_op=1) for i, k in enumerate(served)]
    g.remote_dma_fused(out, local_sem=sem.left)

    g.sync.wait_ge(sem.ag, NB)
    g.sync.dma_start(T.y[:], T.agland[:]).then_inc(sem.stored, 16)
    g.wait_ge(sem.left, 2 * NB)
    g.sync.wait_ge(sem.stored, 16)
